import numpy as np
import ml_dtypes


def mxq(x, axis, fmt="e4m3"):
    dtype, down = {"e4m3": (ml_dtypes.float8_e4m3fn, 7), "e5m2": (ml_dtypes.float8_e5m2, 14)}[fmt]
    v = np.moveaxis(np.asarray(x, np.float32).astype(ml_dtypes.bfloat16).astype(np.float64), axis, -1)
    blocks = v.reshape(v.shape[:-1] + (-1, 32))
    amax = np.abs(blocks).max(-1, keepdims=True)
    byte = np.maximum(np.where(amax > 0, np.frexp(amax)[1] - 1 + 127, 0) - down, 1)
    scale = np.exp2(byte - 127.0)
    codes = (blocks / scale).astype(np.float32).astype(dtype).astype(np.float64)
    return np.moveaxis((codes * scale).reshape(v.shape), -1, axis)


WIDE = False


def mx_kscale(k):
    if not WIDE:
        return np.ones(k)
    levels = np.array([10, -10, 5, -5, 0])
    if k % 512:
        return np.exp2(np.random.permutation(np.resize(levels, k // 32))).repeat(32)
    a = np.empty((k // 512, 16))
    for p in range(k // 512):
        a[p, :8] = np.random.permutation(np.resize(levels, 8))
        for g in range(8):
            far = levels[np.abs(levels - a[p, g]) >= 10]
            a[p, g + 8] = far[np.random.randint(len(far))]
    return np.exp2(a.ravel()).repeat(32)


def f64(x):
    return np.asarray(x).astype(np.float64)


def striped(idx):
    return np.tile(idx.reshape(-1, 16).T, (8, 1)).astype(np.uint16)


def unstriped(offs):
    return offs[:16].T.reshape(-1).astype(np.int64)


def pack_weight(w):
    k, n = w.shape
    w = f64(np.asarray(w, np.float32).astype(ml_dtypes.bfloat16)).reshape(k // 32, 32, n)
    amax = np.abs(w).max(1)
    byte = np.clip(np.where(amax > 0, np.frexp(amax)[1] - 1 + 127 - 7, 1), 1, 254)
    scaled = (w * np.exp2(127.0 - byte)[:, None, :]).reshape(k, n).astype(np.float32)
    words = np.ascontiguousarray(scaled.reshape(k // 512, 128, 4, n).transpose(0, 1, 3, 2)).astype(ml_dtypes.float8_e4m3fn).view(np.uint8)
    return words, np.ascontiguousarray(byte.astype(np.uint8).reshape(k // 512, 16, n))


def unpack_weight(words, scales):
    g, p, n, _ = words.shape
    vals = np.ascontiguousarray(words).view(ml_dtypes.float8_e4m3fn).astype(np.float64) * np.repeat(np.exp2(scales.astype(np.float64) - 127.0), 8, axis=1)[..., None]
    return vals.transpose(0, 1, 3, 2).reshape(g * 512, n)


K, T, S, D, N, V = 512, 4096, 1024, 8, 128, 128


def setup_inputs():
    n = np.random.standard_normal
    s = mx_kscale(K)[:, None]
    packed_xT = pack_weight(n((K, T)) * s)
    return {
        "x_words": packed_xT[0],
        "x_scales": packed_xT[1],
        "w1": (n((K, N)) / np.sqrt(K) / s).astype(np.float32),
        "w2": (n((K, N)) / np.sqrt(K) / s).astype(np.float32),
        "ilam": (-np.random.uniform(0.8, 3.0, (N, 1))).astype(np.float32),
        "eps": (n((N, S))).astype(np.float32),
        "ctrl": (n((N, V))).astype(np.float32),
        "offs": striped(np.random.permutation(T)[:S]),
    }


def reference(x_words, x_scales, w1, w2, ilam, eps, ctrl, offs):
    xq = unpack_weight(x_words, x_scales)[:, unstriped(offs)]
    yc = mxq(f64(w1), 0, "e4m3").T @ xq
    yd = mxq(f64(w2), 0, "e4m3").T @ xq
    cost = np.log(np.exp(yc) + 1.0) + 0.3 * ((yd) ** 2)
    least = cost.reshape(len(cost), -1, D).min(axis=2)
    wt = np.exp(f64(ilam) * (cost - np.repeat(least, D, axis=1)))
    we = wt * f64(eps)
    tw = wt.reshape(len(wt), -1, D).sum(axis=2)
    du = (we.reshape(len(we), -1, D).sum(axis=2)) / tw
    nu = f64(ctrl) + du
    return 0.25 * (np.pad(nu, ((0, 0), (1, 0)))[:, :V] + np.pad(nu, ((0, 0), (0, 1)))[:, 1:]) + 0.5 * nu

@@ -1,0 +1,144 @@
+from contextlib import ExitStack
+import math
+
+import concourse.mybir as mybir
+
+F32 = mybir.dt.float32
+BF16 = mybir.dt.bfloat16
+I32 = mybir.dt.int32
+U32 = mybir.dt.uint32
+U16 = mybir.dt.uint16
+U8 = mybir.dt.uint8
+FP8X4 = mybir.dt.float8_e4m3fn_x4
+ALU = mybir.AluOpType
+ACT = mybir.ActivationFunctionType
+AX = mybir.AxisListType
+
+P = 128
+K, T, S, D, M, V = 512, 4096, 1024, 8, 128, 128
+FLOPS = 2 * 2 * K * M * S
+CH = 256
+NCH = S // CH
+CUTS = [0,64,128,192,256]
+LATE = [0,128,256]
+LAST = [0,256]
+KNEE = 16.0
+SOFTPLUS_KNEE = KNEE + math.log(1.0 + math.exp(-KNEE))
+TINY = 2.0 ** -63
+
+
+def tile_picked_ymppi_upd_p_kernel(tc, x_words, x_scales, w1, w2, ilam, eps, ctrl, offs, out):
+    nc = tc.nc
+    with ExitStack() as ctx:
+        keep = ctx.enter_context(tc.tile_pool(name="keep", bufs=1))
+        psum = ctx.enter_context(tc.psum_pool(name="psum", bufs=1))
+
+        offsets = keep.tile([P, S // 16], U16, name="offsets")
+        scale_table = keep.tile([P, T], U8, name="scale_table", tag="chain", align_bytes=64)
+        word_table = keep.tile([P, T], U32, name="word_table", align_bytes=64)
+        w_raw = [keep.tile([P, 4, M], F32, name=f"w_raw{i}") for i in range(2)]
+        eps_sb = keep.tile([P, S], F32, name="eps_sb")
+        ctrl_sb = keep.tile([P, V], F32, name="ctrl_sb")
+        ilam_sb = keep.tile([P, 1], F32, name="ilam_sb")
+
+        nc.gpsimd.memset(scale_table[:, 0 : 2048].bitcast(I32), 0)
+        nc.vector.memset(scale_table[:, 2048 : T].bitcast(I32), 0)
+        nc.sync.dma_start(offsets[:], offs)
+        nc.scalar.dma_start(scale_table[0:P:8, :].bitcast(I32), x_scales[0].bitcast(I32))
+        for i, w in enumerate((w1, w2)):
+            nc.sync.dma_start(w_raw[i][:], w.rearrange("(p j) m -> p j m", j=4))
+        nc.sync.dma_start(word_table[:].bitcast(I32), x_words[0].rearrange("p n t -> p (n t)").bitcast(I32))
+        nc.sync.dma_start(ctrl_sb[:], ctrl)
+        nc.sync.dma_start(eps_sb[:], eps)
+        nc.sync.dma_start(ilam_sb[:], ilam)
+
+        picked_scales = keep.tile([P, S], U8, name="picked_scales", align_bytes=64)
+        nc.vector.tensor_copy(picked_scales[:], scale_table[:].indirect(offsets[:]))
+        x_plane = keep.tile([P, S], U8, name="x_plane", align_bytes=64)
+        nc.gpsimd.memset(x_plane[:].bitcast(I32), 0)
+        for r in range(4):
+            nc.scalar.dma_start(x_plane[r:P:32, :].bitcast(I32), picked_scales[8 * r : P : 32, :].bitcast(I32))
+
+        w_bf = keep.tile([P, 2, M, 4], BF16, name="w_bf", tag="chain", align_bytes=64)
+        w_codes = keep.tile([P, 2 * M], U32, name="w_codes", align_bytes=64)
+        w_plane = keep.tile([P, 2 * M], U8, name="w_plane", align_bytes=64)
+        for i in range(2):
+            nc.vector.tensor_copy(w_bf[:, i], w_raw[i][:].rearrange("p j m -> p m j"))
+        nc.vector.quantize_mx(out=w_codes[:].bitcast(FP8X4), scales=w_plane[:], in_=w_bf[:].rearrange("p i m j -> p (i m j)"))
+
+        sig = keep.tile([P, NCH, CH], F32, name="sig")
+        base = keep.tile([P, NCH, CH], F32, name="base")
+        yc = [psum.tile([P, CH], F32, name=f"yc{c}") for c in range(NCH)]
+        yd = [psum.tile([P, CH], F32, name=f"yd{c}") for c in range(NCH)]
+        sq = [keep.tile([P, CH], F32, name=f"sq{c}") for c in range(NCH)]
+        picked_words = keep.tile([P, S], U32, name="picked_words", tag="chain", align_bytes=64)
+        for c in range(NCH):
+            picked = picked_words[:, c * CH : (c + 1) * CH]
+            nc.vector.tensor_copy(picked, word_table[:].indirect(offsets[:, c * CH // 16 : (c + 1) * CH // 16]))
+            for i, acc in enumerate((yc[c], yd[c])):
+                nc.tensor.matmul_mx(
+                    out=acc[:],
+                    lhsT=w_codes[:, i * M : (i + 1) * M].bitcast(FP8X4),
+                    lhsT_scale=w_plane[:, i * M : (i + 1) * M],
+                    rhs=picked.bitcast(FP8X4),
+                    rhs_scale=x_plane[:, c * CH : (c + 1) * CH],
+                    start=True,
+                    stop=True,
+                )
+            nc.scalar.activation(sig[:, c, :], yc[c][:], ACT.Sigmoid, scale=-1.0)
+            if c < NCH - 1:
+                nc.scalar.activation(sq[c][:], yd[c][:], ACT.Square, scale=math.sqrt(0.3))
+            else:
+                scaled = keep.tile([P, CH], F32, name=f"scaled{c}")
+                nc.vector.tensor_scalar(scaled[:], yd[c][:], 0.3, None, ALU.mult)
+                nc.vector.tensor_tensor(sq[c][:], yd[c][:], scaled[:], ALU.mult)
+        for c in range(NCH):
+            nc.vector.scalar_tensor_tensor(base[:, c, :], yc[c][:], KNEE, sq[c][:], ALU.max, ALU.add)
+
+        G = CH // D
+        shifted = keep.tile([P, NCH, CH], F32, name="shifted")
+        nc.gpsimd.tensor_tensor(
+            shifted[:].rearrange("p c (v d) -> p (c v) d", d=D),
+            eps_sb[:].rearrange("p (v d) -> p v d", d=D),
+            ctrl_sb[:].unsqueeze(2).to_broadcast([P, V, D]),
+            ALU.add,
+        )
+        quarter = keep.tile([P, V + 2], F32, name="quarter")
+        nc.gpsimd.memset(quarter[:], 0.0)
+
+        parts = list(zip(CUTS[:-1], CUTS[1:]))
+        logs = [keep.tile([P, NCH, b - a], F32, name=f"log{a}") for a, b in parts]
+        gains = [keep.tile([P, NCH, b - a], F32, name=f"gain{a}") for a, b in parts]
+        gaps = [keep.tile([P, NCH, b - a], F32, name=f"gap{a}") for a, b in parts]
+        tops = [keep.tile([P, NCH * (b - a) // D], F32, name=f"top{a}") for a, b in parts]
+        wt = keep.tile([P, NCH, CH], F32, name="wt")
+        we = keep.tile([P, NCH, CH], F32, name="we")
+        total_w = keep.tile([P, NCH, G], F32, name="total_w")
+        total_we = keep.tile([P, NCH, G], F32, name="total_we")
+        for k, (a, b) in enumerate(parts):
+            nc.scalar.activation(logs[k][:], sig[:, :, a:b], ACT.Ln, bias=TINY)
+        groups = lambda t: t[:].rearrange("p c (v d) -> p (c v) d", d=D)
+        for k, (a, b) in enumerate(parts):
+            nc.vector.scalar_tensor_tensor(gains[k][:], logs[k][:], -SOFTPLUS_KNEE, base[:, :, a:b], ALU.max, ALU.subtract)
+            nc.vector.tensor_reduce(tops[k][:], groups(gains[k]), AX.X, ALU.max)
+            nc.vector.tensor_tensor(groups(gaps[k]), tops[k][:].unsqueeze(2).to_broadcast([P, NCH * (b - a) // D, D]), groups(gains[k]), ALU.subtract)
+        for k, (a, b) in enumerate(parts):
+            nc.scalar.activation(wt[:, :, a:b], gaps[k][:], ACT.Exp, scale=ilam_sb[:])
+        by_group = lambda t, a, b: t[:, :, a:b].rearrange("p c (v d) -> p c v d", d=D)
+        late = list(zip(LATE[:-1], LATE[1:]))
+        for a, b in late:
+            nc.vector.tensor_tensor(we[:, :, a:b], wt[:, :, a:b], shifted[:, :, a:b], ALU.mult)
+            nc.vector.tensor_reduce(total_w[:, :, a // D : b // D], by_group(wt, a, b), AX.X, ALU.add)
+        for a, b in list(zip(LAST[:-1], LAST[1:])):
+            nc.vector.tensor_reduce(total_we[:, :, a // D : b // D], by_group(we, a, b), AX.X, ALU.add)
+
+        inv = keep.tile([P, V], F32, name="inv")
+        root = keep.tile([P, V], F32, name="root")
+        nc.scalar.activation(root[:], total_w[:].rearrange("p c v -> p (c v)"), ACT.Abs_reciprocal_sqrt)
+        nc.scalar.activation(inv[:], root[:], ACT.Square, scale=0.5)
+        nc.vector.tensor_tensor(quarter[:, 1 : V + 1], total_we[:].rearrange("p c v -> p (c v)"), inv[:], ALU.mult)
+        pairs = keep.tile([P, V + 1], F32, name="pairs")
+        result = keep.tile([P, V], F32, name="result")
+        nc.vector.tensor_tensor(pairs[:], quarter[:, 0 : V + 1], quarter[:, 1 : V + 2], ALU.add)
+        nc.vector.tensor_tensor(result[:], pairs[:, 0:V], pairs[:, 1 : V + 1], ALU.add)
+        nc.sync.dma_start(out, result[:])

@@ -44,13 +44,13 @@ def tile_picked_ymppi_upd_p_kernel(tc, x_words, x_scales, w1, w2, ilam, eps, ctr
         nc.gpsimd.memset(scale_table[:, 0 : 2048].bitcast(I32), 0)
         nc.vector.memset(scale_table[:, 2048 : T].bitcast(I32), 0)
         nc.sync.dma_start(offsets[:], offs)
+        nc.sync.dma_start(ilam_sb[:], ilam)
         nc.scalar.dma_start(scale_table[0:P:8, :].bitcast(I32), x_scales[0].bitcast(I32))
         for i, w in enumerate((w1, w2)):
             nc.sync.dma_start(w_raw[i][:], w.rearrange("(p j) m -> p j m", j=4))
         nc.sync.dma_start(word_table[:].bitcast(I32), x_words[0].rearrange("p n t -> p (n t)").bitcast(I32))
         nc.sync.dma_start(ctrl_sb[:], ctrl)
         nc.sync.dma_start(eps_sb[:], eps)
-        nc.sync.dma_start(ilam_sb[:], ilam)
 
         picked_scales = keep.tile([P, S], U8, name="picked_scales", align_bytes=64)
         nc.vector.tensor_copy(picked_scales[:], scale_table[:].indirect(offsets[:]))
@@ -96,8 +96,8 @@ def tile_picked_ymppi_upd_p_kernel(tc, x_words, x_scales, w1, w2, ilam, eps, ctr
             nc.vector.scalar_tensor_tensor(base[:, c, :], yc[c][:], KNEE, sq[c][:], ALU.max, ALU.add)
 
         G = CH // D
-        shifted = keep.tile([P, NCH, CH], F32, name="shifted")
-        nc.gpsimd.tensor_tensor(
+        shifted = keep.tile([P, NCH, CH], F32, name="shifted", tag="chain", align_bytes=64)
+        nc.vector.tensor_tensor(
             shifted[:].rearrange("p c (v d) -> p (c v) d", d=D),
             eps_sb[:].rearrange("p (v d) -> p v d", d=D),
             ctrl_sb[:].unsqueeze(2).to_broadcast([P, V, D]),

@@ -37,29 +37,29 @@ def tile_picked_ymppi_upd_p_kernel(tc, x_words, x_scales, w1, w2, ilam, eps, ctr
         scale_table = keep.tile([P, T], U8, name="scale_table", tag="chain", align_bytes=64)
         word_table = keep.tile([P, T], U32, name="word_table", align_bytes=64)
         w_raw = [keep.tile([P, 4, M], F32, name=f"w_raw{i}") for i in range(2)]
-        eps_sb = keep.tile([P, S], F32, name="eps_sb")
         ctrl_sb = keep.tile([P, V], F32, name="ctrl_sb")
         ilam_sb = keep.tile([P, 1], F32, name="ilam_sb")
 
-        nc.gpsimd.memset(scale_table[:, 0 : 2048].bitcast(I32), 0)
-        nc.vector.memset(scale_table[:, 2048 : T].bitcast(I32), 0)
+        nc.gpsimd.memset(scale_table[:, 0 : 2560].bitcast(I32), 0)
+        nc.vector.memset(scale_table[:, 2560 : T].bitcast(I32), 0)
         nc.sync.dma_start(offsets[:], offs)
-        nc.sync.dma_start(ilam_sb[:], ilam)
-        nc.scalar.dma_start(scale_table[0:P:8, :].bitcast(I32), x_scales[0].bitcast(I32))
-        for i, w in enumerate((w1, w2)):
-            nc.sync.dma_start(w_raw[i][:], w.rearrange("(p j) m -> p j m", j=4))
+        nc.sync.dma_start(w_raw[0][:], w1.rearrange("(p j) m -> p j m", j=4))
+        nc.sync.dma_start(scale_table[0:P:8, :].bitcast(I32), x_scales[0].bitcast(I32))
+        nc.sync.dma_start(w_raw[1][:], w2.rearrange("(p j) m -> p j m", j=4))
         nc.sync.dma_start(word_table[:].bitcast(I32), x_words[0].rearrange("p n t -> p (n t)").bitcast(I32))
+        nc.sync.dma_start(ilam_sb[:], ilam)
         nc.sync.dma_start(ctrl_sb[:], ctrl)
-        nc.sync.dma_start(eps_sb[:], eps)
 
         picked_scales = keep.tile([P, S], U8, name="picked_scales", align_bytes=64)
         nc.vector.tensor_copy(picked_scales[:], scale_table[:].indirect(offsets[:]))
         x_plane = keep.tile([P, S], U8, name="x_plane", align_bytes=64)
         nc.gpsimd.memset(x_plane[:].bitcast(I32), 0)
         for r in range(4):
-            nc.scalar.dma_start(x_plane[r:P:32, :].bitcast(I32), picked_scales[8 * r : P : 32, :].bitcast(I32))
+            nc.sync.dma_start(x_plane[r:P:32, :].bitcast(I32), picked_scales[8 * r : P : 32, :].bitcast(I32))
 
-        w_bf = keep.tile([P, 2, M, 4], BF16, name="w_bf", tag="chain", align_bytes=64)
+        eps_sb = keep.tile([P, S], F32, name="eps_sb", tag="chain", align_bytes=64)
+        nc.sync.dma_start(eps_sb[:], eps)
+        w_bf = keep.tile([P, 2, M, 4], BF16, name="w_bf", align_bytes=64)
         w_codes = keep.tile([P, 2 * M], U32, name="w_codes", align_bytes=64)
         w_plane = keep.tile([P, 2 * M], U8, name="w_plane", align_bytes=64)
         for i in range(2):
@@ -71,7 +71,7 @@ def tile_picked_ymppi_upd_p_kernel(tc, x_words, x_scales, w1, w2, ilam, eps, ctr
         yc = [psum.tile([P, CH], F32, name=f"yc{c}") for c in range(NCH)]
         yd = [psum.tile([P, CH], F32, name=f"yd{c}") for c in range(NCH)]
         sq = [keep.tile([P, CH], F32, name=f"sq{c}") for c in range(NCH)]
-        picked_words = keep.tile([P, S], U32, name="picked_words", tag="chain", align_bytes=64)
+        picked_words = keep.tile([P, S], U32, name="picked_words", align_bytes=64)
         for c in range(NCH):
             picked = picked_words[:, c * CH : (c + 1) * CH]
             nc.vector.tensor_copy(picked, word_table[:].indirect(offsets[:, c * CH // 16 : (c + 1) * CH // 16]))
@@ -96,7 +96,7 @@ def tile_picked_ymppi_upd_p_kernel(tc, x_words, x_scales, w1, w2, ilam, eps, ctr
             nc.vector.scalar_tensor_tensor(base[:, c, :], yc[c][:], KNEE, sq[c][:], ALU.max, ALU.add)
 
         G = CH // D
-        shifted = keep.tile([P, NCH, CH], F32, name="shifted", tag="chain", align_bytes=64)
+        shifted = keep.tile([P, NCH, CH], F32, name="shifted")
         nc.vector.tensor_tensor(
             shifted[:].rearrange("p c (v d) -> p (c v) d", d=D),
             eps_sb[:].rearrange("p (v d) -> p v d", d=D),

@@ -22,6 +22,7 @@ NCH = S // CH
 CUTS = [0,64,128,192,256]
 LATE = [0,128,256]
 LAST = [0,256]
+SPLIT = 112
 KNEE = 16.0
 SOFTPLUS_KNEE = KNEE + math.log(1.0 + math.exp(-KNEE))
 TINY = 2.0 ** -63
@@ -31,14 +32,13 @@ def tile_picked_ymppi_upd_p_kernel(tc, x_words, x_scales, w1, w2, ilam, eps, ctr
     nc = tc.nc
     with ExitStack() as ctx:
         keep = ctx.enter_context(tc.tile_pool(name="keep", bufs=1))
+        shared = ctx.enter_context(tc.tile_pool(name="shared", bufs=1))
         psum = ctx.enter_context(tc.psum_pool(name="psum", bufs=1))
 
         offsets = keep.tile([P, S // 16], U16, name="offsets")
-        scale_table = keep.tile([P, T], U8, name="scale_table", tag="chain", align_bytes=64)
-        word_table = keep.tile([P, T], U32, name="word_table", align_bytes=64)
+        scale_table = shared.tile([P, T], U8, name="scale_table", offset=0, align_bytes=64)
+        word_table = keep.tile([P, T], U32, name="word_table", tag="words", align_bytes=64)
         w_raw = [keep.tile([P, 4, M], F32, name=f"w_raw{i}") for i in range(2)]
-        ctrl_sb = keep.tile([P, V], F32, name="ctrl_sb")
-        ilam_sb = keep.tile([P, 1], F32, name="ilam_sb")
 
         nc.gpsimd.memset(scale_table[:, 0 : 2560].bitcast(I32), 0)
         nc.vector.memset(scale_table[:, 2560 : T].bitcast(I32), 0)
@@ -47,8 +47,6 @@ def tile_picked_ymppi_upd_p_kernel(tc, x_words, x_scales, w1, w2, ilam, eps, ctr
         nc.sync.dma_start(scale_table[0:P:8, :].bitcast(I32), x_scales[0].bitcast(I32))
         nc.sync.dma_start(w_raw[1][:], w2.rearrange("(p j) m -> p j m", j=4))
         nc.sync.dma_start(word_table[:].bitcast(I32), x_words[0].rearrange("p n t -> p (n t)").bitcast(I32))
-        nc.sync.dma_start(ilam_sb[:], ilam)
-        nc.sync.dma_start(ctrl_sb[:], ctrl)
 
         picked_scales = keep.tile([P, S], U8, name="picked_scales", align_bytes=64)
         nc.vector.tensor_copy(picked_scales[:], scale_table[:].indirect(offsets[:]))
@@ -57,8 +55,12 @@ def tile_picked_ymppi_upd_p_kernel(tc, x_words, x_scales, w1, w2, ilam, eps, ctr
         for r in range(4):
             nc.sync.dma_start(x_plane[r:P:32, :].bitcast(I32), picked_scales[8 * r : P : 32, :].bitcast(I32))
 
-        eps_sb = keep.tile([P, S], F32, name="eps_sb", tag="chain", align_bytes=64)
+        ctrl_sb = shared.tile([P, V], F32, name="ctrl_sb", offset=0)
+        ilam_sb = shared.tile([P, 1], F32, name="ilam_sb", offset=4 * V)
+        eps_sb = shared.tile([P, S], F32, name="eps_sb", offset=8 * V)
+        nc.sync.dma_start(ctrl_sb[:], ctrl)
         nc.sync.dma_start(eps_sb[:], eps)
+        nc.sync.dma_start(ilam_sb[:], ilam)
         w_bf = keep.tile([P, 2, M, 4], BF16, name="w_bf", align_bytes=64)
         w_codes = keep.tile([P, 2 * M], U32, name="w_codes", align_bytes=64)
         w_plane = keep.tile([P, 2 * M], U8, name="w_plane", align_bytes=64)
@@ -86,7 +88,7 @@ def tile_picked_ymppi_upd_p_kernel(tc, x_words, x_scales, w1, w2, ilam, eps, ctr
                     stop=True,
                 )
             nc.scalar.activation(sig[:, c, :], yc[c][:], ACT.Sigmoid, scale=-1.0)
-            if c < NCH - 1:
+            if c < NCH - 2:
                 nc.scalar.activation(sq[c][:], yd[c][:], ACT.Square, scale=math.sqrt(0.3))
             else:
                 scaled = keep.tile([P, CH], F32, name=f"scaled{c}")
@@ -96,8 +98,8 @@ def tile_picked_ymppi_upd_p_kernel(tc, x_words, x_scales, w1, w2, ilam, eps, ctr
             nc.vector.scalar_tensor_tensor(base[:, c, :], yc[c][:], KNEE, sq[c][:], ALU.max, ALU.add)
 
         G = CH // D
-        shifted = keep.tile([P, NCH, CH], F32, name="shifted")
-        nc.vector.tensor_tensor(
+        shifted = keep.tile([P, NCH, CH], F32, name="shifted", tag="words", align_bytes=64)
+        nc.gpsimd.tensor_tensor(
             shifted[:].rearrange("p c (v d) -> p (c v) d", d=D),
             eps_sb[:].rearrange("p (v d) -> p v d", d=D),
             ctrl_sb[:].unsqueeze(2).to_broadcast([P, V, D]),
@@ -118,24 +120,31 @@ def tile_picked_ymppi_upd_p_kernel(tc, x_words, x_scales, w1, w2, ilam, eps, ctr
         for k, (a, b) in enumerate(parts):
             nc.scalar.activation(logs[k][:], sig[:, :, a:b], ACT.Ln, bias=TINY)
         groups = lambda t: t[:].rearrange("p c (v d) -> p (c v) d", d=D)
-        for k, (a, b) in enumerate(parts):
-            nc.vector.scalar_tensor_tensor(gains[k][:], logs[k][:], -SOFTPLUS_KNEE, base[:, :, a:b], ALU.max, ALU.subtract)
-            nc.vector.tensor_reduce(tops[k][:], groups(gains[k]), AX.X, ALU.max)
-            nc.vector.tensor_tensor(groups(gaps[k]), tops[k][:].unsqueeze(2).to_broadcast([P, NCH * (b - a) // D, D]), groups(gains[k]), ALU.subtract)
+        for step in range(len(parts) + 2):
+            if step < len(parts):
+                a, b = parts[step]
+                nc.vector.scalar_tensor_tensor(gains[step][:], logs[step][:], -SOFTPLUS_KNEE, base[:, :, a:b], ALU.max, ALU.subtract)
+            if 0 <= step - 1 < len(parts):
+                nc.vector.tensor_reduce(tops[step - 1][:], groups(gains[step - 1]), AX.X, ALU.max)
+            if 0 <= step - 2 < len(parts):
+                k = step - 2
+                a, b = parts[k]
+                nc.vector.tensor_tensor(groups(gaps[k]), tops[k][:].unsqueeze(2).to_broadcast([P, NCH * (b - a) // D, D]), groups(gains[k]), ALU.subtract)
         for k, (a, b) in enumerate(parts):
             nc.scalar.activation(wt[:, :, a:b], gaps[k][:], ACT.Exp, scale=ilam_sb[:])
         by_group = lambda t, a, b: t[:, :, a:b].rearrange("p c (v d) -> p c v d", d=D)
-        late = list(zip(LATE[:-1], LATE[1:]))
-        for a, b in late:
-            nc.vector.tensor_tensor(we[:, :, a:b], wt[:, :, a:b], shifted[:, :, a:b], ALU.mult)
+        nc.vector.tensor_tensor(we[:, :, 0:SPLIT], wt[:, :, 0:SPLIT], shifted[:, :, 0:SPLIT], ALU.mult)
+        nc.gpsimd.tensor_tensor(we[:, :, SPLIT:CH], wt[:, :, SPLIT:CH], shifted[:, :, SPLIT:CH], ALU.mult)
+        for a, b in ((0, CH // 2), (CH // 2, CH)):
             nc.vector.tensor_reduce(total_w[:, :, a // D : b // D], by_group(wt, a, b), AX.X, ALU.add)
-        for a, b in list(zip(LAST[:-1], LAST[1:])):
-            nc.vector.tensor_reduce(total_we[:, :, a // D : b // D], by_group(we, a, b), AX.X, ALU.add)
+        root = keep.tile([P, V], F32, name="root")
+        flat_w = total_w[:].rearrange("p c v -> p (c v)")
+        nc.vector.tensor_reduce(total_we[:, :, 0 : SPLIT // D], by_group(we, 0, SPLIT), AX.X, ALU.add)
+        nc.vector.tensor_tensor(root[:], flat_w, flat_w, ALU.mult)
+        nc.vector.tensor_reduce(total_we[:, :, SPLIT // D : G], by_group(we, SPLIT, CH), AX.X, ALU.add)
 
         inv = keep.tile([P, V], F32, name="inv")
-        root = keep.tile([P, V], F32, name="root")
-        nc.scalar.activation(root[:], total_w[:].rearrange("p c v -> p (c v)"), ACT.Abs_reciprocal_sqrt)
-        nc.scalar.activation(inv[:], root[:], ACT.Square, scale=0.5)
+        nc.scalar.activation(inv[:], root[:], ACT.Abs_reciprocal_sqrt, scale=16.0)
         nc.vector.tensor_tensor(quarter[:, 1 : V + 1], total_we[:].rearrange("p c v -> p (c v)"), inv[:], ALU.mult)
         pairs = keep.tile([P, V + 1], F32, name="pairs")
         result = keep.tile([P, V], F32, name="result")

@@ -17,135 +17,155 @@ AX = mybir.AxisListType
 P = 128
 K, T, S, D, M, V = 512, 4096, 1024, 8, 128, 128
 FLOPS = 2 * 2 * K * M * S
-CH = 256
-NCH = S // CH
-CUTS = [0,64,128,192,256]
-LATE = [0,128,256]
-LAST = [0,256]
+PACK = 4
+LIST_ROWS = 16
+
+CHUNK = 256
+CHUNKS = S // CHUNK
+GROUPS = CHUNK // D
+PART = 64
+PARTS = CHUNK // PART
+SCALAR_SQUARES = 2
 SPLIT = 112
+
 KNEE = 16.0
 SOFTPLUS_KNEE = KNEE + math.log(1.0 + math.exp(-KNEE))
 TINY = 2.0 ** -63
+
+CTRL_AT, ILAM_AT, ROUNDED_AT, EPS_AT = 0, 512, 1024, 3072
+
+
+def groups_of(tile):
+    return tile[:].rearrange("p c (v d) -> p (c v) d", d=D)
+
+
+def groups_in(tile, first, last):
+    return tile[:, :, first:last].rearrange("p c (v d) -> p c v d", d=D)
 
 
 def tile_picked_ymppi_upd_p_kernel(tc, x_words, x_scales, w1, w2, ilam, eps, ctrl, offs, out):
     nc = tc.nc
     with ExitStack() as ctx:
         keep = ctx.enter_context(tc.tile_pool(name="keep", bufs=1))
-        shared = ctx.enter_context(tc.tile_pool(name="shared", bufs=1))
+        reuse = ctx.enter_context(tc.tile_pool(name="reuse", bufs=1))
         psum = ctx.enter_context(tc.psum_pool(name="psum", bufs=1))
 
-        offsets = keep.tile([P, S // 16], U16, name="offsets")
-        scale_table = shared.tile([P, T], U8, name="scale_table", offset=0, align_bytes=64)
+        offsets = keep.tile([P, S // LIST_ROWS], U16, name="offsets")
+        scale_table = reuse.tile([P, T], U8, name="scale_table", offset=0, align_bytes=64)
         word_table = keep.tile([P, T], U32, name="word_table", tag="words", align_bytes=64)
-        w_raw = [keep.tile([P, 4, M], F32, name=f"w_raw{i}") for i in range(2)]
-
-        nc.gpsimd.memset(scale_table[:, 0 : 2560].bitcast(I32), 0)
-        nc.vector.memset(scale_table[:, 2560 : T].bitcast(I32), 0)
+        w_raw = [keep.tile([P, PACK, M], F32, name=f"w_raw{i}") for i in range(2)]
+        nc.vector.memset(scale_table[:].bitcast(I32), 0)
         nc.sync.dma_start(offsets[:], offs)
-        nc.sync.dma_start(w_raw[0][:], w1.rearrange("(p j) m -> p j m", j=4))
+        nc.sync.dma_start(w_raw[0][:], w1.rearrange("(p j) m -> p j m", j=PACK))
         nc.sync.dma_start(scale_table[0:P:8, :].bitcast(I32), x_scales[0].bitcast(I32))
-        nc.sync.dma_start(w_raw[1][:], w2.rearrange("(p j) m -> p j m", j=4))
+        nc.sync.dma_start(w_raw[1][:], w2.rearrange("(p j) m -> p j m", j=PACK))
         nc.sync.dma_start(word_table[:].bitcast(I32), x_words[0].rearrange("p n t -> p (n t)").bitcast(I32))
 
         picked_scales = keep.tile([P, S], U8, name="picked_scales", align_bytes=64)
         nc.vector.tensor_copy(picked_scales[:], scale_table[:].indirect(offsets[:]))
         x_plane = keep.tile([P, S], U8, name="x_plane", align_bytes=64)
-        nc.gpsimd.memset(x_plane[:].bitcast(I32), 0)
+        nc.vector.memset(x_plane[:].bitcast(I32), 0)
         for r in range(4):
             nc.sync.dma_start(x_plane[r:P:32, :].bitcast(I32), picked_scales[8 * r : P : 32, :].bitcast(I32))
 
-        ctrl_sb = shared.tile([P, V], F32, name="ctrl_sb", offset=0)
-        ilam_sb = shared.tile([P, 1], F32, name="ilam_sb", offset=4 * V)
-        eps_sb = shared.tile([P, S], F32, name="eps_sb", offset=8 * V)
+        ctrl_sb = reuse.tile([P, V], F32, name="ctrl_sb", offset=CTRL_AT)
+        ilam_sb = reuse.tile([P, 1], F32, name="ilam_sb", offset=ILAM_AT)
+        eps_sb = reuse.tile([P, S], F32, name="eps_sb", offset=EPS_AT)
         nc.sync.dma_start(ctrl_sb[:], ctrl)
         nc.sync.dma_start(eps_sb[:], eps)
         nc.sync.dma_start(ilam_sb[:], ilam)
-        w_bf = keep.tile([P, 2, M, 4], BF16, name="w_bf", align_bytes=64)
+
+        w_rounded = reuse.tile([P, 2, M, PACK], BF16, name="w_rounded", offset=ROUNDED_AT, align_bytes=64)
         w_codes = keep.tile([P, 2 * M], U32, name="w_codes", align_bytes=64)
         w_plane = keep.tile([P, 2 * M], U8, name="w_plane", align_bytes=64)
         for i in range(2):
-            nc.vector.tensor_copy(w_bf[:, i], w_raw[i][:].rearrange("p j m -> p m j"))
-        nc.vector.quantize_mx(out=w_codes[:].bitcast(FP8X4), scales=w_plane[:], in_=w_bf[:].rearrange("p i m j -> p (i m j)"))
+            nc.vector.tensor_copy(w_rounded[:, i], w_raw[i][:].rearrange("p j m -> p m j"))
+        nc.vector.quantize_mx(
+            out=w_codes[:].bitcast(FP8X4), scales=w_plane[:], in_=w_rounded[:].rearrange("p i m j -> p (i m j)")
+        )
 
-        sig = keep.tile([P, NCH, CH], F32, name="sig")
-        base = keep.tile([P, NCH, CH], F32, name="base")
-        yc = [psum.tile([P, CH], F32, name=f"yc{c}") for c in range(NCH)]
-        yd = [psum.tile([P, CH], F32, name=f"yd{c}") for c in range(NCH)]
-        sq = [keep.tile([P, CH], F32, name=f"sq{c}") for c in range(NCH)]
+        sig = keep.tile([P, CHUNKS, CHUNK], F32, name="sig")
+        base = keep.tile([P, CHUNKS, CHUNK], F32, name="base")
+        yc = [psum.tile([P, CHUNK], F32, name=f"yc{c}") for c in range(CHUNKS)]
+        yd = [psum.tile([P, CHUNK], F32, name=f"yd{c}") for c in range(CHUNKS)]
+        square = [keep.tile([P, CHUNK], F32, name=f"square{c}") for c in range(CHUNKS)]
         picked_words = keep.tile([P, S], U32, name="picked_words", align_bytes=64)
-        for c in range(NCH):
-            picked = picked_words[:, c * CH : (c + 1) * CH]
-            nc.vector.tensor_copy(picked, word_table[:].indirect(offsets[:, c * CH // 16 : (c + 1) * CH // 16]))
-            for i, acc in enumerate((yc[c], yd[c])):
+        for c in range(CHUNKS):
+            entries = slice(c * CHUNK, (c + 1) * CHUNK)
+            list_columns = slice(c * CHUNK // LIST_ROWS, (c + 1) * CHUNK // LIST_ROWS)
+            nc.vector.tensor_copy(picked_words[:, entries], word_table[:].indirect(offsets[:, list_columns]))
+            for i, product in enumerate((yc[c], yd[c])):
                 nc.tensor.matmul_mx(
-                    out=acc[:],
+                    out=product[:],
                     lhsT=w_codes[:, i * M : (i + 1) * M].bitcast(FP8X4),
                     lhsT_scale=w_plane[:, i * M : (i + 1) * M],
-                    rhs=picked.bitcast(FP8X4),
-                    rhs_scale=x_plane[:, c * CH : (c + 1) * CH],
+                    rhs=picked_words[:, entries].bitcast(FP8X4),
+                    rhs_scale=x_plane[:, entries],
                     start=True,
                     stop=True,
                 )
             nc.scalar.activation(sig[:, c, :], yc[c][:], ACT.Sigmoid, scale=-1.0)
-            if c < NCH - 2:
-                nc.scalar.activation(sq[c][:], yd[c][:], ACT.Square, scale=math.sqrt(0.3))
+            if c < SCALAR_SQUARES:
+                nc.scalar.activation(square[c][:], yd[c][:], ACT.Square, scale=math.sqrt(0.3))
             else:
-                scaled = keep.tile([P, CH], F32, name=f"scaled{c}")
+                scaled = keep.tile([P, CHUNK], F32, name=f"scaled{c}")
                 nc.vector.tensor_scalar(scaled[:], yd[c][:], 0.3, None, ALU.mult)
-                nc.vector.tensor_tensor(sq[c][:], yd[c][:], scaled[:], ALU.mult)
-        for c in range(NCH):
-            nc.vector.scalar_tensor_tensor(base[:, c, :], yc[c][:], KNEE, sq[c][:], ALU.max, ALU.add)
+                nc.vector.tensor_tensor(square[c][:], yd[c][:], scaled[:], ALU.mult)
+        for c in range(CHUNKS):
+            nc.vector.scalar_tensor_tensor(base[:, c, :], yc[c][:], KNEE, square[c][:], ALU.max, ALU.add)
 
-        G = CH // D
-        shifted = keep.tile([P, NCH, CH], F32, name="shifted", tag="words", align_bytes=64)
+        shifted = keep.tile([P, CHUNKS, CHUNK], F32, name="shifted", tag="words", align_bytes=64)
         nc.gpsimd.tensor_tensor(
-            shifted[:].rearrange("p c (v d) -> p (c v) d", d=D),
+            groups_of(shifted),
             eps_sb[:].rearrange("p (v d) -> p v d", d=D),
             ctrl_sb[:].unsqueeze(2).to_broadcast([P, V, D]),
             ALU.add,
         )
         quarter = keep.tile([P, V + 2], F32, name="quarter")
-        nc.gpsimd.memset(quarter[:], 0.0)
+        nc.vector.memset(quarter[:, 0 : V + 2 : V + 1], 0.0)
 
-        parts = list(zip(CUTS[:-1], CUTS[1:]))
-        logs = [keep.tile([P, NCH, b - a], F32, name=f"log{a}") for a, b in parts]
-        gains = [keep.tile([P, NCH, b - a], F32, name=f"gain{a}") for a, b in parts]
-        gaps = [keep.tile([P, NCH, b - a], F32, name=f"gap{a}") for a, b in parts]
-        tops = [keep.tile([P, NCH * (b - a) // D], F32, name=f"top{a}") for a, b in parts]
-        wt = keep.tile([P, NCH, CH], F32, name="wt")
-        we = keep.tile([P, NCH, CH], F32, name="we")
-        total_w = keep.tile([P, NCH, G], F32, name="total_w")
-        total_we = keep.tile([P, NCH, G], F32, name="total_we")
-        for k, (a, b) in enumerate(parts):
-            nc.scalar.activation(logs[k][:], sig[:, :, a:b], ACT.Ln, bias=TINY)
-        groups = lambda t: t[:].rearrange("p c (v d) -> p (c v) d", d=D)
-        for step in range(len(parts) + 2):
-            if step < len(parts):
-                a, b = parts[step]
-                nc.vector.scalar_tensor_tensor(gains[step][:], logs[step][:], -SOFTPLUS_KNEE, base[:, :, a:b], ALU.max, ALU.subtract)
-            if 0 <= step - 1 < len(parts):
-                nc.vector.tensor_reduce(tops[step - 1][:], groups(gains[step - 1]), AX.X, ALU.max)
-            if 0 <= step - 2 < len(parts):
-                k = step - 2
-                a, b = parts[k]
-                nc.vector.tensor_tensor(groups(gaps[k]), tops[k][:].unsqueeze(2).to_broadcast([P, NCH * (b - a) // D, D]), groups(gains[k]), ALU.subtract)
-        for k, (a, b) in enumerate(parts):
-            nc.scalar.activation(wt[:, :, a:b], gaps[k][:], ACT.Exp, scale=ilam_sb[:])
-        by_group = lambda t, a, b: t[:, :, a:b].rearrange("p c (v d) -> p c v d", d=D)
+        columns = [slice(n * PART, (n + 1) * PART) for n in range(PARTS)]
+        part_groups = CHUNKS * PART // D
+        logs = [keep.tile([P, CHUNKS, PART], F32, name=f"log{n}") for n in range(PARTS)]
+        gains = [keep.tile([P, CHUNKS, PART], F32, name=f"gain{n}") for n in range(PARTS)]
+        gaps = [keep.tile([P, CHUNKS, PART], F32, name=f"gap{n}") for n in range(PARTS)]
+        tops = [keep.tile([P, part_groups], F32, name=f"top{n}") for n in range(PARTS)]
+        wt = keep.tile([P, CHUNKS, CHUNK], F32, name="wt")
+        we = keep.tile([P, CHUNKS, CHUNK], F32, name="we")
+        total_wt = keep.tile([P, CHUNKS, GROUPS], F32, name="total_wt")
+        total_we = keep.tile([P, CHUNKS, GROUPS], F32, name="total_we")
+
+        for n in range(PARTS):
+            nc.scalar.activation(logs[n][:], sig[:, :, columns[n]], ACT.Ln, bias=TINY)
+        for step in range(PARTS + 2):
+            if step < PARTS:
+                n = step
+                nc.vector.scalar_tensor_tensor(
+                    gains[n][:], logs[n][:], -SOFTPLUS_KNEE, base[:, :, columns[n]], ALU.max, ALU.subtract
+                )
+            if 1 <= step <= PARTS:
+                n = step - 1
+                nc.vector.tensor_reduce(tops[n][:], groups_of(gains[n]), AX.X, ALU.max)
+            if step >= 2:
+                n = step - 2
+                top_for_each = tops[n][:].unsqueeze(2).to_broadcast([P, part_groups, D])
+                nc.vector.tensor_tensor(groups_of(gaps[n]), top_for_each, groups_of(gains[n]), ALU.subtract)
+        for n in range(PARTS):
+            nc.scalar.activation(wt[:, :, columns[n]], gaps[n][:], ACT.Exp, scale=ilam_sb[:])
+
         nc.vector.tensor_tensor(we[:, :, 0:SPLIT], wt[:, :, 0:SPLIT], shifted[:, :, 0:SPLIT], ALU.mult)
-        nc.gpsimd.tensor_tensor(we[:, :, SPLIT:CH], wt[:, :, SPLIT:CH], shifted[:, :, SPLIT:CH], ALU.mult)
-        for a, b in ((0, CH // 2), (CH // 2, CH)):
-            nc.vector.tensor_reduce(total_w[:, :, a // D : b // D], by_group(wt, a, b), AX.X, ALU.add)
-        root = keep.tile([P, V], F32, name="root")
-        flat_w = total_w[:].rearrange("p c v -> p (c v)")
-        nc.vector.tensor_reduce(total_we[:, :, 0 : SPLIT // D], by_group(we, 0, SPLIT), AX.X, ALU.add)
-        nc.vector.tensor_tensor(root[:], flat_w, flat_w, ALU.mult)
-        nc.vector.tensor_reduce(total_we[:, :, SPLIT // D : G], by_group(we, SPLIT, CH), AX.X, ALU.add)
+        nc.gpsimd.tensor_tensor(we[:, :, SPLIT:CHUNK], wt[:, :, SPLIT:CHUNK], shifted[:, :, SPLIT:CHUNK], ALU.mult)
+        for first, last in ((0, CHUNK // 2), (CHUNK // 2, CHUNK)):
+            nc.vector.tensor_reduce(total_wt[:, :, first // D : last // D], groups_in(wt, first, last), AX.X, ALU.add)
+        total_squared = keep.tile([P, V], F32, name="total_squared")
+        total_by_time = total_wt[:].rearrange("p c v -> p (c v)")
+        nc.vector.tensor_reduce(total_we[:, :, 0 : SPLIT // D], groups_in(we, 0, SPLIT), AX.X, ALU.add)
+        nc.vector.tensor_tensor(total_squared[:], total_by_time, total_by_time, ALU.mult)
+        nc.vector.tensor_reduce(total_we[:, :, SPLIT // D : GROUPS], groups_in(we, SPLIT, CHUNK), AX.X, ALU.add)
 
-        inv = keep.tile([P, V], F32, name="inv")
-        nc.scalar.activation(inv[:], root[:], ACT.Abs_reciprocal_sqrt, scale=16.0)
-        nc.vector.tensor_tensor(quarter[:, 1 : V + 1], total_we[:].rearrange("p c v -> p (c v)"), inv[:], ALU.mult)
+        inverse = keep.tile([P, V], F32, name="inverse")
+        nc.scalar.activation(inverse[:], total_squared[:], ACT.Abs_reciprocal_sqrt, scale=16.0)
+        nc.vector.tensor_tensor(quarter[:, 1 : V + 1], total_we[:].rearrange("p c v -> p (c v)"), inverse[:], ALU.mult)
         pairs = keep.tile([P, V + 1], F32, name="pairs")
         result = keep.tile([P, V], F32, name="result")
         nc.vector.tensor_tensor(pairs[:], quarter[:, 0 : V + 1], quarter[:, 1 : V + 2], ALU.add)

from contextlib import ExitStack
import math

import concourse.mybir as mybir

F32 = mybir.dt.float32
BF16 = mybir.dt.bfloat16
I32 = mybir.dt.int32
U32 = mybir.dt.uint32
U16 = mybir.dt.uint16
U8 = mybir.dt.uint8
FP8X4 = mybir.dt.float8_e4m3fn_x4
ALU = mybir.AluOpType
ACT = mybir.ActivationFunctionType
AX = mybir.AxisListType

P = 128
K, T, S, D, M, V = 512, 4096, 1024, 8, 128, 128
FLOPS = 2 * 2 * K * M * S
PACK = 4
LIST_ROWS = 16

CHUNK = 256
CHUNKS = S // CHUNK
GROUPS = CHUNK // D
PART = 64
PARTS = CHUNK // PART
SCALAR_SQUARES = 2
SPLIT = 112

KNEE = 16.0
SOFTPLUS_KNEE = KNEE + math.log(1.0 + math.exp(-KNEE))
TINY = 2.0 ** -63

CTRL_AT, ILAM_AT, ROUNDED_AT, EPS_AT = 0, 512, 1024, 3072


def groups_of(tile):
    return tile[:].rearrange("p c (v d) -> p (c v) d", d=D)


def groups_in(tile, first, last):
    return tile[:, :, first:last].rearrange("p c (v d) -> p c v d", d=D)


def tile_picked_ymppi_upd_p_kernel(tc, x_words, x_scales, w1, w2, ilam, eps, ctrl, offs, out):
    nc = tc.nc
    with ExitStack() as ctx:
        keep = ctx.enter_context(tc.tile_pool(name="keep", bufs=1))
        reuse = ctx.enter_context(tc.tile_pool(name="reuse", bufs=1))
        psum = ctx.enter_context(tc.psum_pool(name="psum", bufs=1))

        offsets = keep.tile([P, S // LIST_ROWS], U16, name="offsets")
        scale_table = reuse.tile([P, T], U8, name="scale_table", offset=0, align_bytes=64)
        word_table = keep.tile([P, T], U32, name="word_table", tag="words", align_bytes=64)
        w_raw = [keep.tile([P, PACK, M], F32, name=f"w_raw{i}") for i in range(2)]
        nc.vector.memset(scale_table[:].bitcast(I32), 0)
        nc.sync.dma_start(offsets[:], offs)
        nc.sync.dma_start(w_raw[0][:], w1.rearrange("(p j) m -> p j m", j=PACK))
        nc.sync.dma_start(scale_table[0:P:8, :].bitcast(I32), x_scales[0].bitcast(I32))
        nc.sync.dma_start(w_raw[1][:], w2.rearrange("(p j) m -> p j m", j=PACK))
        nc.sync.dma_start(word_table[:].bitcast(I32), x_words[0].rearrange("p n t -> p (n t)").bitcast(I32))

        picked_scales = keep.tile([P, S], U8, name="picked_scales", align_bytes=64)
        nc.vector.tensor_copy(picked_scales[:], scale_table[:].indirect(offsets[:]))
        x_plane = keep.tile([P, S], U8, name="x_plane", align_bytes=64)
        nc.vector.memset(x_plane[:].bitcast(I32), 0)
        for r in range(4):
            nc.sync.dma_start(x_plane[r:P:32, :].bitcast(I32), picked_scales[8 * r : P : 32, :].bitcast(I32))

        ctrl_sb = reuse.tile([P, V], F32, name="ctrl_sb", offset=CTRL_AT)
        ilam_sb = reuse.tile([P, 1], F32, name="ilam_sb", offset=ILAM_AT)
        eps_sb = reuse.tile([P, S], F32, name="eps_sb", offset=EPS_AT)
        nc.sync.dma_start(ctrl_sb[:], ctrl)
        nc.sync.dma_start(eps_sb[:], eps)
        nc.sync.dma_start(ilam_sb[:], ilam)

        w_rounded = reuse.tile([P, 2, M, PACK], BF16, name="w_rounded", offset=ROUNDED_AT, align_bytes=64)
        w_codes = keep.tile([P, 2 * M], U32, name="w_codes", align_bytes=64)
        w_plane = keep.tile([P, 2 * M], U8, name="w_plane", align_bytes=64)
        for i in range(2):
            nc.vector.tensor_copy(w_rounded[:, i], w_raw[i][:].rearrange("p j m -> p m j"))
        nc.vector.quantize_mx(
            out=w_codes[:].bitcast(FP8X4), scales=w_plane[:], in_=w_rounded[:].rearrange("p i m j -> p (i m j)")
        )

        sig = keep.tile([P, CHUNKS, CHUNK], F32, name="sig")
        base = keep.tile([P, CHUNKS, CHUNK], F32, name="base")
        yc = [psum.tile([P, CHUNK], F32, name=f"yc{c}") for c in range(CHUNKS)]
        yd = [psum.tile([P, CHUNK], F32, name=f"yd{c}") for c in range(CHUNKS)]
        square = [keep.tile([P, CHUNK], F32, name=f"square{c}") for c in range(CHUNKS)]
        picked_words = keep.tile([P, S], U32, name="picked_words", align_bytes=64)
        for c in range(CHUNKS):
            entries = slice(c * CHUNK, (c + 1) * CHUNK)
            list_columns = slice(c * CHUNK // LIST_ROWS, (c + 1) * CHUNK // LIST_ROWS)
            nc.vector.tensor_copy(picked_words[:, entries], word_table[:].indirect(offsets[:, list_columns]))
            for i, product in enumerate((yc[c], yd[c])):
                nc.tensor.matmul_mx(
                    out=product[:],
                    lhsT=w_codes[:, i * M : (i + 1) * M].bitcast(FP8X4),
                    lhsT_scale=w_plane[:, i * M : (i + 1) * M],
                    rhs=picked_words[:, entries].bitcast(FP8X4),
                    rhs_scale=x_plane[:, entries],
                    start=True,
                    stop=True,
                )
            nc.scalar.activation(sig[:, c, :], yc[c][:], ACT.Sigmoid, scale=-1.0)
            if c < SCALAR_SQUARES:
                nc.scalar.activation(square[c][:], yd[c][:], ACT.Square, scale=math.sqrt(0.3))
            else:
                scaled = keep.tile([P, CHUNK], F32, name=f"scaled{c}")
                nc.vector.tensor_scalar(scaled[:], yd[c][:], 0.3, None, ALU.mult)
                nc.vector.tensor_tensor(square[c][:], yd[c][:], scaled[:], ALU.mult)
        for c in range(CHUNKS):
            nc.vector.scalar_tensor_tensor(base[:, c, :], yc[c][:], KNEE, square[c][:], ALU.max, ALU.add)

        shifted = keep.tile([P, CHUNKS, CHUNK], F32, name="shifted", tag="words", align_bytes=64)
        nc.gpsimd.tensor_tensor(
            groups_of(shifted),
            eps_sb[:].rearrange("p (v d) -> p v d", d=D),
            ctrl_sb[:].unsqueeze(2).to_broadcast([P, V, D]),
            ALU.add,
        )
        quarter = keep.tile([P, V + 2], F32, name="quarter")
        nc.vector.memset(quarter[:, 0 : V + 2 : V + 1], 0.0)

        columns = [slice(n * PART, (n + 1) * PART) for n in range(PARTS)]
        part_groups = CHUNKS * PART // D
        logs = [keep.tile([P, CHUNKS, PART], F32, name=f"log{n}") for n in range(PARTS)]
        gains = [keep.tile([P, CHUNKS, PART], F32, name=f"gain{n}") for n in range(PARTS)]
        gaps = [keep.tile([P, CHUNKS, PART], F32, name=f"gap{n}") for n in range(PARTS)]
        tops = [keep.tile([P, part_groups], F32, name=f"top{n}") for n in range(PARTS)]
        wt = keep.tile([P, CHUNKS, CHUNK], F32, name="wt")
        we = keep.tile([P, CHUNKS, CHUNK], F32, name="we")
        total_wt = keep.tile([P, CHUNKS, GROUPS], F32, name="total_wt")
        total_we = keep.tile([P, CHUNKS, GROUPS], F32, name="total_we")

        for n in range(PARTS):
            nc.scalar.activation(logs[n][:], sig[:, :, columns[n]], ACT.Ln, bias=TINY)
        for step in range(PARTS + 2):
            if step < PARTS:
                n = step
                nc.vector.scalar_tensor_tensor(
                    gains[n][:], logs[n][:], -SOFTPLUS_KNEE, base[:, :, columns[n]], ALU.max, ALU.subtract
                )
            if 1 <= step <= PARTS:
                n = step - 1
                nc.vector.tensor_reduce(tops[n][:], groups_of(gains[n]), AX.X, ALU.max)
            if step >= 2:
                n = step - 2
                top_for_each = tops[n][:].unsqueeze(2).to_broadcast([P, part_groups, D])
                nc.vector.tensor_tensor(groups_of(gaps[n]), top_for_each, groups_of(gains[n]), ALU.subtract)
        for n in range(PARTS):
            nc.scalar.activation(wt[:, :, columns[n]], gaps[n][:], ACT.Exp, scale=ilam_sb[:])

        nc.vector.tensor_tensor(we[:, :, 0:SPLIT], wt[:, :, 0:SPLIT], shifted[:, :, 0:SPLIT], ALU.mult)
        nc.gpsimd.tensor_tensor(we[:, :, SPLIT:CHUNK], wt[:, :, SPLIT:CHUNK], shifted[:, :, SPLIT:CHUNK], ALU.mult)
        for first, last in ((0, CHUNK // 2), (CHUNK // 2, CHUNK)):
            nc.vector.tensor_reduce(total_wt[:, :, first // D : last // D], groups_in(wt, first, last), AX.X, ALU.add)
        total_squared = keep.tile([P, V], F32, name="total_squared")
        total_by_time = total_wt[:].rearrange("p c v -> p (c v)")
        nc.vector.tensor_reduce(total_we[:, :, 0 : SPLIT // D], groups_in(we, 0, SPLIT), AX.X, ALU.add)
        nc.vector.tensor_tensor(total_squared[:], total_by_time, total_by_time, ALU.mult)
        nc.vector.tensor_reduce(total_we[:, :, SPLIT // D : GROUPS], groups_in(we, SPLIT, CHUNK), AX.X, ALU.add)

        inverse = keep.tile([P, V], F32, name="inverse")
        nc.scalar.activation(inverse[:], total_squared[:], ACT.Abs_reciprocal_sqrt, scale=16.0)
        nc.vector.tensor_tensor(quarter[:, 1 : V + 1], total_we[:].rearrange("p c v -> p (c v)"), inverse[:], ALU.mult)
        pairs = keep.tile([P, V + 1], F32, name="pairs")
        result = keep.tile([P, V], F32, name="result")
        nc.vector.tensor_tensor(pairs[:], quarter[:, 0 : V + 1], quarter[:, 1 : V + 2], ALU.add)
        nc.vector.tensor_tensor(result[:], pairs[:, 0:V], pairs[:, 1 : V + 1], ALU.add)
        nc.sync.dma_start(out, result[:])
